import numpy as np
import ml_dtypes


def mxq(x, axis, fmt="e4m3"):
    dtype, down = {"e4m3": (ml_dtypes.float8_e4m3fn, 7), "e5m2": (ml_dtypes.float8_e5m2, 14)}[fmt]
    v = np.moveaxis(np.asarray(x, np.float32).astype(ml_dtypes.bfloat16).astype(np.float64), axis, -1)
    blocks = v.reshape(v.shape[:-1] + (-1, 32))
    amax = np.abs(blocks).max(-1, keepdims=True)
    byte = np.maximum(np.where(amax > 0, np.frexp(amax)[1] - 1 + 127, 0) - down, 1)
    scale = np.exp2(byte - 127.0)
    codes = (blocks / scale).astype(np.float32).astype(dtype).astype(np.float64)
    return np.moveaxis((codes * scale).reshape(v.shape), -1, axis)


WIDE = False


def mx_kscale(k):
    if not WIDE:
        return np.ones(k)
    levels = np.array([10, -10, 5, -5, 0])
    if k % 512:
        return np.exp2(np.random.permutation(np.resize(levels, k // 32))).repeat(32)
    a = np.empty((k // 512, 16))
    for p in range(k // 512):
        a[p, :8] = np.random.permutation(np.resize(levels, 8))
        for g in range(8):
            far = levels[np.abs(levels - a[p, g]) >= 10]
            a[p, g + 8] = far[np.random.randint(len(far))]
    return np.exp2(a.ravel()).repeat(32)


def f64(x):
    return np.asarray(x).astype(np.float64)


def striped(idx):
    return np.tile(idx.reshape(-1, 16).T, (8, 1)).astype(np.uint16)


def unstriped(offs):
    return offs[:16].T.reshape(-1).astype(np.int64)


def pack_weight(w):
    k, n = w.shape
    w = f64(np.asarray(w, np.float32).astype(ml_dtypes.bfloat16)).reshape(k // 32, 32, n)
    amax = np.abs(w).max(1)
    byte = np.clip(np.where(amax > 0, np.frexp(amax)[1] - 1 + 127 - 7, 1), 1, 254)
    scaled = (w * np.exp2(127.0 - byte)[:, None, :]).reshape(k, n).astype(np.float32)
    words = np.ascontiguousarray(scaled.reshape(k // 512, 128, 4, n).transpose(0, 1, 3, 2)).astype(ml_dtypes.float8_e4m3fn).view(np.uint8)
    return words, np.ascontiguousarray(byte.astype(np.uint8).reshape(k // 512, 16, n))


def unpack_weight(words, scales):
    g, p, n, _ = words.shape
    vals = np.ascontiguousarray(words).view(ml_dtypes.float8_e4m3fn).astype(np.float64) * np.repeat(np.exp2(scales.astype(np.float64) - 127.0), 8, axis=1)[..., None]
    return vals.transpose(0, 1, 3, 2).reshape(g * 512, n)


def relu(v):
    return np.maximum(v, 0.0)


K, T, S, H, Z, A = 1024, 4096, 1024, 512, 128, 512


def setup_inputs():
    n = np.random.standard_normal
    s = mx_kscale(K)[:, None]
    u = mx_kscale(H)
    packed_xT = pack_weight(n((K, T)) * s)
    return {
        "x_words": packed_xT[0],
        "x_scales": packed_xT[1],
        "w1": (n((K, H)) / np.sqrt(K) / s * u).astype(np.float32),
        "wv": (n((H, Z)) / np.sqrt(H) / u[:, None]).astype(np.float32),
        "wa": (n((H, A)) / np.sqrt(H) / u[:, None]).astype(np.float32),
        "offs": striped(np.random.permutation(T)[:S]),
    }


def reference(x_words, x_scales, w1, wv, wa, offs):
    xq = unpack_weight(x_words, x_scales)[:, unstriped(offs)]
    h = relu(mxq(f64(w1), 0, "e4m3").T @ xq)
    hq = mxq(h, 0, "e4m3")
    wvq = mxq(f64(wv), 0, "e4m3")
    vv = hq.T @ wvq
    waq = mxq(f64(wa), 0, "e4m3")
    a = hq.T @ waq
    a0 = a[:, :Z]
    a1 = a[:, Z:2 * Z]
    a2 = a[:, 2 * Z:3 * Z]
    a3 = a[:, 3 * Z:4 * Z]
    mean = 0.25 * (a0 + a1 + a2 + a3)
    return vv + np.maximum(np.maximum(np.maximum(a0, a1), a2), a3) - mean

@@ -1,0 +1,210 @@
+from contextlib import ExitStack
+
+import concourse.mybir as mybir
+
+K, T, S, H, Z, A = 1024, 4096, 1024, 512, 128, 512
+FLOPS = 2 * K * H * S + 2 * H * S * (Z + A)
+
+F32 = mybir.dt.float32
+BF16 = mybir.dt.bfloat16
+I32 = mybir.dt.int32
+U32 = mybir.dt.uint32
+U16 = mybir.dt.uint16
+U8 = mybir.dt.uint8
+FP8X4 = mybir.dt.float8_e4m3fn_x4
+ALU = mybir.AluOpType
+ACT = mybir.ActivationFunctionType
+
+P = 128
+PACK = 4
+K_PASS = P * PACK
+PASSES = K // K_PASS
+TILES = S // P
+PAIRS = TILES // 2
+HALF = H // 2
+HEAD_BANKS = ((0, 1, 2), (3, 0, 1), (4, 5, 2), (6, 7, 3))
+VECTOR_SHARE = 44
+
+
+def tile_picked_yduel_max_p_kernel(tc, x_words, x_scales, w1, wv, wa, offs, out):
+    nc = tc.nc
+    with ExitStack() as ctx:
+        keep = ctx.enter_context(tc.tile_pool(name="keep", bufs=1))
+        ring = ctx.enter_context(tc.tile_pool(name="ring", bufs=2))
+        psum = ctx.enter_context(tc.psum_pool(name="psum", bufs=1))
+
+        def load_rows(name, rows):
+            raw = keep.tile([P, PACK, rows.shape[1]], F32, name=name)
+            nc.sync.dma_start(out=raw[:], in_=rows.rearrange("(p j) c -> p j c", j=PACK))
+            return raw
+
+        def load_words(words, g, cols):
+            src = x_words[g].rearrange("p n r -> p (n r)").bitcast(I32)
+            nc.sync.dma_start(out=words[:, cols].bitcast(I32), in_=src[:, cols])
+
+        def load_scales(blocks):
+            for g, q in blocks:
+                nc.sync.dma_start(
+                    out=scale_window[32 * q + 4 * g : 32 * q + 4 * g + 4, :].bitcast(I32),
+                    in_=x_scales[g, 4 * q : 4 * q + 4, :].bitcast(I32),
+                )
+
+        offsets = keep.tile([P, S // 16], U16, name="offsets")
+        nc.sync.dma_start(offsets[:], offs)
+
+        scale_window = keep.tile([P, T], U8, name="scale_window")
+        nc.vector.memset(scale_window[:, 0 : T // 2].bitcast(I32), 0)
+        nc.gpsimd.memset(scale_window[:, T // 2 : T].bitcast(I32), 0)
+
+        scale_blocks = [(g, q) for g in range(PASSES) for q in range(4)]
+        x_window = [keep.tile([P, T], U32, name="x_window%d" % g) for g in range(PASSES)]
+        load_words(x_window[0], 0, slice(0, T // 2))
+        load_scales(scale_blocks[:6])
+        load_words(x_window[0], 0, slice(T // 2, T))
+        load_scales(scale_blocks[6:])
+        w1_first = load_rows("w1_raw0", w1[0:K_PASS, :])
+        load_words(x_window[1], 1, slice(0, T))
+        w1_raw = [
+            [w1_first],
+            [load_rows("w1_raw1%d" % u, w1[K_PASS:K, u * HALF : (u + 1) * HALF]) for u in range(2)],
+        ]
+        wv_raw = load_rows("wv_raw", wv)
+        wa_raw = [load_rows("wa_raw%d" % u, wa[:, u * HALF : (u + 1) * HALF]) for u in range(2)]
+
+        def gather(name, window, dtype):
+            picked = keep.tile([P, S], dtype, name=name, align_bytes=64)
+            nc.vector.tensor_copy(picked[:], window[:].indirect(offsets[:]))
+            return picked
+
+        def quantize(name, values, width, step):
+            codes = keep.tile([P, width], U32, name=name + "_codes", align_bytes=64)
+            scales = keep.tile([P, width], U8, name=name + "_scales", align_bytes=64)
+            for c in range(0, width, step):
+                nc.vector.quantize_mx(
+                    out=codes[:, c : c + step].bitcast(FP8X4),
+                    scales=scales[:, c : c + step],
+                    in_=values[:, PACK * c : PACK * (c + step)],
+                )
+            return codes, scales
+
+        def prepare_w1(g):
+            grouped = keep.tile([P, H * PACK], BF16, name="w1_grouped%d" % g, align_bytes=64)
+            dst = grouped[:].rearrange("p (t m j) -> p m t j", t=PACK, j=PACK)
+            src = [raw[:].rearrange("p j (m t) -> p m t j", t=PACK) for raw in w1_raw[g]]
+            if g == 0:
+                nc.scalar.copy(out=dst, in_=src[0])
+            else:
+                nc.scalar.copy(out=dst[:, 0 : P // 2], in_=src[0])
+                nc.vector.tensor_copy(out=dst[:, P // 2 : P // 2 + VECTOR_SHARE], in_=src[1][:, 0:VECTOR_SHARE])
+                nc.scalar.copy(out=dst[:, P // 2 + VECTOR_SHARE : P], in_=src[1][:, VECTOR_SHARE : P // 2])
+            return quantize("w1q%d" % g, grouped, H, P if g == PASSES - 1 else H)
+
+        def interleaved(grouped, raw):
+            return (
+                grouped[:].rearrange("p (c i j) -> p c j i", i=4, j=PACK),
+                raw[:].rearrange("p j (c i) -> p c j i", i=4),
+            )
+
+        def prepare_wv():
+            wv_grouped = keep.tile([P, Z * PACK], BF16, name="wv_grouped", align_bytes=64)
+            dst, src = interleaved(wv_grouped, wv_raw)
+            nc.scalar.activation(out=dst, in_=src, func=ACT.Copy, scale=-4.0)
+            return quantize("wvq", wv_grouped, Z, Z)
+
+        x_scale = gather("x_scale", scale_window, U8)
+        hidden = [psum.tile([P, PACK, P], F32, name="hidden%d" % i, tag="bank%d" % i) for i in range(TILES)]
+        for g in range(PASSES):
+            x_codes = gather("x_codes%d" % g, x_window[g], U32)
+            w1_codes, w1_scales = prepare_w1(g)
+            for i in range(TILES):
+                tokens = slice(i * P, (i + 1) * P)
+                for t in range(PACK):
+                    cols = slice(t * P, (t + 1) * P)
+                    nc.tensor.matmul_mx(
+                        out=hidden[i][:, t, :],
+                        lhsT=w1_codes[:, cols].bitcast(FP8X4),
+                        lhsT_scale=w1_scales[:, cols],
+                        rhs=x_codes[:, tokens].bitcast(FP8X4),
+                        rhs_scale=x_scale[4 * g : P, tokens],
+                        start=(g == 0 and t == 0),
+                        stop=(g == PASSES - 1 and t == PACK - 1),
+                    )
+
+        def cast_wa(u):
+            grouped = keep.tile([P, HALF * PACK], BF16, name="wa_grouped%d" % u, align_bytes=64)
+            dst, src = interleaved(grouped, wa_raw[u])
+            nc.vector.tensor_copy(out=dst, in_=src)
+            return grouped
+
+        def quantize_hidden(k):
+            h_bf = keep.tile([P, 2 * P * PACK], BF16, name="h_bf%d" % k, align_bytes=64)
+            for j in range(2):
+                nc.scalar.activation(
+                    out=h_bf[:, j * P * PACK : (j + 1) * P * PACK].rearrange("p (n t) -> p n t", t=PACK),
+                    in_=hidden[2 * k + j][:].rearrange("p t n -> p n t"),
+                    func=ACT.Relu,
+                )
+            return quantize("hq%d" % k, h_bf, 2 * P, 2 * P)
+
+        def heads(k, h_codes, h_scales):
+            adv = [
+                psum.tile([P, 2, HALF], F32, name="adv%d%d" % (k, u), tag="bank%d" % HEAD_BANKS[k][u])
+                for u in range(2)
+            ]
+            rest = psum.tile([P, 2, Z], F32, name="rest%d" % k, tag="bank%d" % HEAD_BANKS[k][2])
+
+            def product(dst, j, operand, cols, start, stop):
+                tokens = slice(j * P, (j + 1) * P)
+                codes, scales = operand
+                nc.tensor.matmul_mx(
+                    out=dst,
+                    lhsT=h_codes[:, tokens].bitcast(FP8X4),
+                    lhsT_scale=h_scales[:, tokens],
+                    rhs=codes[:, cols].bitcast(FP8X4),
+                    rhs_scale=scales[:, cols],
+                    start=start,
+                    stop=stop,
+                )
+
+            for u in range(2):
+                for j in range(2):
+                    product(adv[u][:, j, :], j, wa_q[u], slice(0, HALF), True, True)
+            terms = [
+                ((wv_codes, wv_scales), slice(0, Z)),
+                (wa_q[0], slice(Z, 2 * Z)),
+                (wa_q[1], slice(0, Z)),
+                (wa_q[1], slice(Z, 2 * Z)),
+            ]
+            if k == PAIRS - 1:
+                terms.append((wa_q[0], slice(0, Z)))
+            for j in range(2):
+                for n, (operand, cols) in enumerate(terms):
+                    product(rest[:, j, :], j, operand, cols, n == 0, n == len(terms) - 1)
+
+            low = ring.tile([P, 2, HALF], F32, name="low")
+            nc.scalar.copy(out=low[:], in_=adv[0][:])
+            wide_max = ring.tile([P, 2, HALF], F32, name="wide_max")
+            nc.vector.tensor_tensor(wide_max[:], adv[1][:], low[:], ALU.max)
+            total = rest
+            if k < PAIRS - 1:
+                total = ring.tile([P, 2, Z], F32, name="total")
+                nc.vector.tensor_tensor(total[:], rest[:], low[:, :, 0:Z], ALU.add)
+            best = ring.tile([P, 2, Z], F32, name="best")
+            nc.vector.tensor_tensor(best[:], wide_max[:, :, 0:Z], wide_max[:, :, Z : 2 * Z], ALU.max)
+            result = ring.tile([P, 2, Z], F32, name="result", bufs=PAIRS)
+            nc.vector.scalar_tensor_tensor(result[:], total[:], -0.25, best[:], ALU.mult, ALU.add)
+            nc.sync.dma_start(
+                out=out[2 * k * P : 2 * (k + 1) * P, :].rearrange("(j p) z -> p j z", p=P),
+                in_=result[:],
+            )
+
+        wv_codes, wv_scales = prepare_wv()
+        wa_q = [quantize("waq0", cast_wa(0), HALF, HALF)]
+        wa_last = cast_wa(1)
+        h_q = [quantize_hidden(0)]
+        wa_q.append(quantize("waq1", wa_last, HALF, HALF))
+        h_q.append(quantize_hidden(1))
+        for k in range(PAIRS):
+            heads(k, *h_q[k])
+            if k + 2 < PAIRS:
+                h_q.append(quantize_hidden(k + 2))

@@ -34,7 +34,7 @@ def tile_picked_yduel_max_p_kernel(tc, x_words, x_scales, w1, wv, wa, offs, out)
         psum = ctx.enter_context(tc.psum_pool(name="psum", bufs=1))
 
         def load_rows(name, rows):
-            raw = keep.tile([P, PACK, rows.shape[1]], F32, name=name)
+            raw = keep.tile([P, PACK, rows.shape[1]], F32, name=name, align_bytes=64)
             nc.sync.dma_start(out=raw[:], in_=rows.rearrange("(p j) c -> p j c", j=PACK))
             return raw
 
@@ -43,10 +43,10 @@ def tile_picked_yduel_max_p_kernel(tc, x_words, x_scales, w1, wv, wa, offs, out)
             nc.sync.dma_start(out=words[:, cols].bitcast(I32), in_=src[:, cols])
 
         def load_scales(blocks):
-            for g, q in blocks:
+            for r, g in blocks:
                 nc.sync.dma_start(
-                    out=scale_window[32 * q + 4 * g : 32 * q + 4 * g + 4, :].bitcast(I32),
-                    in_=x_scales[g, 4 * q : 4 * q + 4, :].bitcast(I32),
+                    out=scale_window[4 * g + r : P : 32, :].bitcast(I32),
+                    in_=x_scales[g, r:16:4, :].bitcast(I32),
                 )
 
         offsets = keep.tile([P, S // 16], U16, name="offsets")
@@ -56,7 +56,7 @@ def tile_picked_yduel_max_p_kernel(tc, x_words, x_scales, w1, wv, wa, offs, out)
         nc.vector.memset(scale_window[:, 0 : T // 2].bitcast(I32), 0)
         nc.gpsimd.memset(scale_window[:, T // 2 : T].bitcast(I32), 0)
 
-        scale_blocks = [(g, q) for g in range(PASSES) for q in range(4)]
+        scale_blocks = [(r, g) for r in range(4) for g in range(PASSES)]
         x_window = [keep.tile([P, T], U32, name="x_window%d" % g) for g in range(PASSES)]
         load_words(x_window[0], 0, slice(0, T // 2))
         load_scales(scale_blocks[:6])
@@ -76,8 +76,8 @@ def tile_picked_yduel_max_p_kernel(tc, x_words, x_scales, w1, wv, wa, offs, out)
             nc.vector.tensor_copy(picked[:], window[:].indirect(offsets[:]))
             return picked
 
-        def quantize(name, values, width, step):
-            codes = keep.tile([P, width], U32, name=name + "_codes", align_bytes=64)
+        def quantize(name, values, width, step, tag=None):
+            codes = keep.tile([P, width], U32, name=name + "_codes", tag=tag or name + "_codes", align_bytes=64)
             scales = keep.tile([P, width], U8, name=name + "_scales", align_bytes=64)
             for c in range(0, width, step):
                 nc.vector.quantize_mx(
@@ -137,14 +137,14 @@ def tile_picked_yduel_max_p_kernel(tc, x_words, x_scales, w1, wv, wa, offs, out)
             return grouped
 
         def quantize_hidden(k):
-            h_bf = keep.tile([P, 2 * P * PACK], BF16, name="h_bf%d" % k, align_bytes=64)
+            h_bf = keep.tile([P, 2 * P * PACK], BF16, name="h_bf%d" % k, tag="h_bf%d" % min(k, 1), align_bytes=64)
             for j in range(2):
                 nc.scalar.activation(
                     out=h_bf[:, j * P * PACK : (j + 1) * P * PACK].rearrange("p (n t) -> p n t", t=PACK),
                     in_=hidden[2 * k + j][:].rearrange("p t n -> p n t"),
                     func=ACT.Relu,
                 )
-            return quantize("hq%d" % k, h_bf, 2 * P, 2 * P)
+            return quantize("hq%d" % k, h_bf, 2 * P, 2 * P, {0: "wa_raw1", 1: "wa_grouped1"}.get(k))
 
         def heads(k, h_codes, h_scales):
             adv = [
@@ -184,22 +184,26 @@ def tile_picked_yduel_max_p_kernel(tc, x_words, x_scales, w1, wv, wa, offs, out)
             low = ring.tile([P, 2, HALF], F32, name="low")
             nc.scalar.copy(out=low[:], in_=adv[0][:])
             wide_max = ring.tile([P, 2, HALF], F32, name="wide_max")
-            nc.vector.tensor_tensor(wide_max[:], adv[1][:], low[:], ALU.max)
+            for part in [slice(0, 2)] if k < PAIRS - 1 else [slice(0, 1), slice(1, 2)]:
+                nc.vector.tensor_tensor(wide_max[:, part], adv[1][:, part], low[:, part], ALU.max)
             total = rest
             if k < PAIRS - 1:
                 total = ring.tile([P, 2, Z], F32, name="total")
                 nc.vector.tensor_tensor(total[:], rest[:], low[:, :, 0:Z], ALU.add)
             best = ring.tile([P, 2, Z], F32, name="best")
-            nc.vector.tensor_tensor(best[:], wide_max[:, :, 0:Z], wide_max[:, :, Z : 2 * Z], ALU.max)
+            for j in range(2):
+                nc.vector.tensor_tensor(best[:, j], wide_max[:, j, 0:Z], wide_max[:, j, Z : 2 * Z], ALU.max)
             result = ring.tile([P, 2, Z], F32, name="result", bufs=PAIRS)
-            nc.vector.scalar_tensor_tensor(result[:], total[:], -0.25, best[:], ALU.mult, ALU.add)
+            for j in range(2):
+                nc.vector.scalar_tensor_tensor(result[:, j], total[:, j], -0.25, best[:, j], ALU.mult, ALU.add)
             nc.sync.dma_start(
                 out=out[2 * k * P : 2 * (k + 1) * P, :].rearrange("(j p) z -> p j z", p=P),
                 in_=result[:],
             )
 
+        wa_first = cast_wa(0)
         wv_codes, wv_scales = prepare_wv()
-        wa_q = [quantize("waq0", cast_wa(0), HALF, HALF)]
+        wa_q = [quantize("waq0", wa_first, HALF, HALF)]
         wa_last = cast_wa(1)
         h_q = [quantize_hidden(0)]
         wa_q.append(quantize("waq1", wa_last, HALF, HALF))

@@ -22,7 +22,7 @@ PASSES = K // K_PASS
 TILES = S // P
 PAIRS = TILES // 2
 HALF = H // 2
-HEAD_BANKS = ((0, 1, 2), (3, 0, 1), (4, 5, 2), (6, 7, 3))
+HEAD_BANKS = ((0, 1, 2), (3, 0, 4), (5, 1, 2), (6, 7, 3))
 VECTOR_SHARE = 44
 
 
@@ -59,10 +59,11 @@ def tile_picked_yduel_max_p_kernel(tc, x_words, x_scales, w1, wv, wa, offs, out)
         scale_blocks = [(r, g) for r in range(4) for g in range(PASSES)]
         x_window = [keep.tile([P, T], U32, name="x_window%d" % g) for g in range(PASSES)]
         load_words(x_window[0], 0, slice(0, T // 2))
-        load_scales(scale_blocks[:6])
+        load_scales(scale_blocks[:5])
         load_words(x_window[0], 0, slice(T // 2, T))
-        load_scales(scale_blocks[6:])
+        load_scales(scale_blocks[5:6])
         w1_first = load_rows("w1_raw0", w1[0:K_PASS, :])
+        load_scales(scale_blocks[6:])
         load_words(x_window[1], 1, slice(0, T))
         w1_raw = [
             [w1_first],
@@ -136,79 +137,110 @@ def tile_picked_yduel_max_p_kernel(tc, x_words, x_scales, w1, wv, wa, offs, out)
             nc.vector.tensor_copy(out=dst, in_=src)
             return grouped
 
-        def quantize_hidden(k):
-            h_bf = keep.tile([P, 2 * P * PACK], BF16, name="h_bf%d" % k, tag="h_bf%d" % min(k, 1), align_bytes=64)
+        def quantize_hidden(k, stage, tag=None):
             for j in range(2):
                 nc.scalar.activation(
-                    out=h_bf[:, j * P * PACK : (j + 1) * P * PACK].rearrange("p (n t) -> p n t", t=PACK),
+                    out=stage[:, j * K_PASS : (j + 1) * K_PASS].rearrange("p (n t) -> p n t", t=PACK),
                     in_=hidden[2 * k + j][:].rearrange("p t n -> p n t"),
                     func=ACT.Relu,
                 )
-            return quantize("hq%d" % k, h_bf, 2 * P, 2 * P, {0: "wa_raw1", 1: "wa_grouped1"}.get(k))
+            h_q.append(quantize("hq%d" % k, stage, 2 * P, 2 * P, tag))
 
-        def heads(k, h_codes, h_scales):
-            adv = [
-                psum.tile([P, 2, HALF], F32, name="adv%d%d" % (k, u), tag="bank%d" % HEAD_BANKS[k][u])
-                for u in range(2)
-            ]
-            rest = psum.tile([P, 2, Z], F32, name="rest%d" % k, tag="bank%d" % HEAD_BANKS[k][2])
-
-            def product(dst, j, operand, cols, start, stop):
+        def products(k, name, bank, width, terms):
+            h_codes, h_scales = h_q[k]
+            acc = psum.tile([P, 2, width], F32, name="%s%d" % (name, k), tag="bank%d" % bank)
+            for j in range(2):
                 tokens = slice(j * P, (j + 1) * P)
-                codes, scales = operand
-                nc.tensor.matmul_mx(
-                    out=dst,
-                    lhsT=h_codes[:, tokens].bitcast(FP8X4),
-                    lhsT_scale=h_scales[:, tokens],
-                    rhs=codes[:, cols].bitcast(FP8X4),
-                    rhs_scale=scales[:, cols],
-                    start=start,
-                    stop=stop,
-                )
+                for n, ((codes, scales), first) in enumerate(terms):
+                    nc.tensor.matmul_mx(
+                        out=acc[:, j, :],
+                        lhsT=h_codes[:, tokens].bitcast(FP8X4),
+                        lhsT_scale=h_scales[:, tokens],
+                        rhs=codes[:, first : first + width].bitcast(FP8X4),
+                        rhs_scale=scales[:, first : first + width],
+                        start=(n == 0),
+                        stop=(n == len(terms) - 1),
+                    )
+            return acc
 
-            for u in range(2):
-                for j in range(2):
-                    product(adv[u][:, j, :], j, wa_q[u], slice(0, HALF), True, True)
-            terms = [
-                ((wv_codes, wv_scales), slice(0, Z)),
-                (wa_q[0], slice(Z, 2 * Z)),
-                (wa_q[1], slice(0, Z)),
-                (wa_q[1], slice(Z, 2 * Z)),
-            ]
+        def front(k):
+            a01[k] = products(k, "a01_", HEAD_BANKS[k][0], HALF, [(wa_q[0], 0)])
+            quarter[k] = keep.tile([P, 2, Z], F32, name="quarter%d" % k)
+            nc.scalar.activation(out=quarter[k][:], in_=a01[k][:, :, 0:Z], func=ACT.Copy, scale=-0.25)
+
+        def back(k):
+            a23[k] = products(k, "a23_", HEAD_BANKS[k][1], HALF, [(wa_q[1], 0)])
+
+        def linear(k):
+            terms = [(wv_q, 0), (wa_q[0], Z), (wa_q[1], 0), (wa_q[1], Z)]
             if k == PAIRS - 1:
-                terms.append((wa_q[0], slice(0, Z)))
-            for j in range(2):
-                for n, (operand, cols) in enumerate(terms):
-                    product(rest[:, j, :], j, operand, cols, n == 0, n == len(terms) - 1)
+                terms.append((wa_q[0], 0))
+            rest[k] = products(k, "rest", HEAD_BANKS[k][2], Z, terms)
 
-            low = ring.tile([P, 2, HALF], F32, name="low")
-            nc.scalar.copy(out=low[:], in_=adv[0][:])
-            wide_max = ring.tile([P, 2, HALF], F32, name="wide_max")
-            for part in [slice(0, 2)] if k < PAIRS - 1 else [slice(0, 1), slice(1, 2)]:
-                nc.vector.tensor_tensor(wide_max[:, part], adv[1][:, part], low[:, part], ALU.max)
-            total = rest
-            if k < PAIRS - 1:
-                total = ring.tile([P, 2, Z], F32, name="total")
-                nc.vector.tensor_tensor(total[:], rest[:], low[:, :, 0:Z], ALU.add)
-            best = ring.tile([P, 2, Z], F32, name="best")
-            for j in range(2):
-                nc.vector.tensor_tensor(best[:, j], wide_max[:, j, 0:Z], wide_max[:, j, Z : 2 * Z], ALU.max)
-            result = ring.tile([P, 2, Z], F32, name="result", bufs=PAIRS)
-            for j in range(2):
-                nc.vector.scalar_tensor_tensor(result[:, j], total[:, j], -0.25, best[:, j], ALU.mult, ALU.add)
+        def max_step(k, action):
+            new = keep.tile([P, 2, Z], F32, name="best%d%d" % (k, action))
+            if action == 1:
+                nc.vector.scalar_tensor_tensor(new[:], quarter[k][:], -4.0, a01[k][:, :, Z : 2 * Z], ALU.mult, ALU.max)
+            else:
+                cols = slice((action - 2) * Z, (action - 1) * Z)
+                nc.vector.tensor_tensor(new[:], a23[k][:, :, cols], best[k][:], ALU.max)
+            best[k] = new
+
+        def shift_of(k):
+            shift[k] = keep.tile([P, 2, Z], F32, name="shift%d" % k)
+            nc.vector.scalar_tensor_tensor(shift[k][:], rest[k][:], -0.25, quarter[k][:], ALU.mult, ALU.add)
+
+        def finish(k):
+            result = keep.tile([P, 2, Z], F32, name="result%d" % k)
+            if k == PAIRS - 1:
+                nc.vector.scalar_tensor_tensor(result[:], rest[k][:], -0.25, best[k][:], ALU.mult, ALU.add)
+            else:
+                nc.vector.tensor_tensor(result[:], best[k][:], shift[k][:], ALU.add)
             nc.sync.dma_start(
                 out=out[2 * k * P : 2 * (k + 1) * P, :].rearrange("(j p) z -> p j z", p=P),
                 in_=result[:],
             )
 
+        h_q, a01, a23, rest, quarter, best, shift = [], {}, {}, {}, {}, {}, {}
         wa_first = cast_wa(0)
-        wv_codes, wv_scales = prepare_wv()
+        wv_q = prepare_wv()
         wa_q = [quantize("waq0", wa_first, HALF, HALF)]
-        wa_last = cast_wa(1)
-        h_q = [quantize_hidden(0)]
-        wa_q.append(quantize("waq1", wa_last, HALF, HALF))
-        h_q.append(quantize_hidden(1))
-        for k in range(PAIRS):
-            heads(k, *h_q[k])
-            if k + 2 < PAIRS:
-                h_q.append(quantize_hidden(k + 2))
+        stage0 = keep.tile([P, 2 * K_PASS], BF16, name="stage0", align_bytes=64)
+        quantize_hidden(0, stage0)
+        front(0)
+        wa_q.append(quantize("waq1", cast_wa(1), HALF, HALF))
+        back(0)
+        linear(0)
+        max_step(0, 1)
+        stage1 = keep.tile([P, 2 * K_PASS], BF16, name="stage1", align_bytes=64)
+        quantize_hidden(1, stage1, "wa_grouped1")
+        front(1)
+        back(1)
+        max_step(0, 2)
+        shift_of(0)
+        max_step(0, 3)
+        max_step(1, 1)
+        finish(0)
+        max_step(1, 2)
+        stage23 = keep.tile([P, 2, 2 * K_PASS], BF16, name="stage23", tag="stage1", align_bytes=64)
+        quantize_hidden(2, stage23[:, 0, :])
+        linear(1)
+        front(2)
+        back(2)
+        max_step(1, 3)
+        shift_of(1)
+        quantize_hidden(3, stage23[:, 1, :])
+        front(3)
+        linear(2)
+        back(3)
+        linear(3)
+        max_step(2, 1)
+        finish(1)
+        max_step(2, 2)
+        max_step(3, 1)
+        max_step(2, 3)
+        max_step(3, 2)
+        shift_of(2)
+        max_step(3, 3)
+        finish(2)
+        finish(3)

from contextlib import ExitStack

import concourse.mybir as mybir

K, T, S, H, Z, A = 1024, 4096, 1024, 512, 128, 512
FLOPS = 2 * K * H * S + 2 * H * S * (Z + A)

F32 = mybir.dt.float32
BF16 = mybir.dt.bfloat16
I32 = mybir.dt.int32
U32 = mybir.dt.uint32
U16 = mybir.dt.uint16
U8 = mybir.dt.uint8
FP8X4 = mybir.dt.float8_e4m3fn_x4
ALU = mybir.AluOpType
ACT = mybir.ActivationFunctionType

P = 128
PACK = 4
K_PASS = P * PACK
PASSES = K // K_PASS
TILES = S // P
PAIRS = TILES // 2
HALF = H // 2
HEAD_BANKS = ((0, 1, 2), (3, 0, 4), (5, 1, 2), (6, 7, 3))
VECTOR_SHARE = 44


def tile_picked_yduel_max_p_kernel(tc, x_words, x_scales, w1, wv, wa, offs, out):
    nc = tc.nc
    with ExitStack() as ctx:
        keep = ctx.enter_context(tc.tile_pool(name="keep", bufs=1))
        ring = ctx.enter_context(tc.tile_pool(name="ring", bufs=2))
        psum = ctx.enter_context(tc.psum_pool(name="psum", bufs=1))

        def load_rows(name, rows):
            raw = keep.tile([P, PACK, rows.shape[1]], F32, name=name, align_bytes=64)
            nc.sync.dma_start(out=raw[:], in_=rows.rearrange("(p j) c -> p j c", j=PACK))
            return raw

        def load_words(words, g, cols):
            src = x_words[g].rearrange("p n r -> p (n r)").bitcast(I32)
            nc.sync.dma_start(out=words[:, cols].bitcast(I32), in_=src[:, cols])

        def load_scales(blocks):
            for r, g in blocks:
                nc.sync.dma_start(
                    out=scale_window[4 * g + r : P : 32, :].bitcast(I32),
                    in_=x_scales[g, r:16:4, :].bitcast(I32),
                )

        offsets = keep.tile([P, S // 16], U16, name="offsets")
        nc.sync.dma_start(offsets[:], offs)

        scale_window = keep.tile([P, T], U8, name="scale_window")
        nc.vector.memset(scale_window[:, 0 : T // 2].bitcast(I32), 0)
        nc.gpsimd.memset(scale_window[:, T // 2 : T].bitcast(I32), 0)

        scale_blocks = [(r, g) for r in range(4) for g in range(PASSES)]
        x_window = [keep.tile([P, T], U32, name="x_window%d" % g) for g in range(PASSES)]
        load_words(x_window[0], 0, slice(0, T // 2))
        load_scales(scale_blocks[:5])
        load_words(x_window[0], 0, slice(T // 2, T))
        load_scales(scale_blocks[5:6])
        w1_first = load_rows("w1_raw0", w1[0:K_PASS, :])
        load_scales(scale_blocks[6:])
        load_words(x_window[1], 1, slice(0, T))
        w1_raw = [
            [w1_first],
            [load_rows("w1_raw1%d" % u, w1[K_PASS:K, u * HALF : (u + 1) * HALF]) for u in range(2)],
        ]
        wv_raw = load_rows("wv_raw", wv)
        wa_raw = [load_rows("wa_raw%d" % u, wa[:, u * HALF : (u + 1) * HALF]) for u in range(2)]

        def gather(name, window, dtype):
            picked = keep.tile([P, S], dtype, name=name, align_bytes=64)
            nc.vector.tensor_copy(picked[:], window[:].indirect(offsets[:]))
            return picked

        def quantize(name, values, width, step, tag=None):
            codes = keep.tile([P, width], U32, name=name + "_codes", tag=tag or name + "_codes", align_bytes=64)
            scales = keep.tile([P, width], U8, name=name + "_scales", align_bytes=64)
            for c in range(0, width, step):
                nc.vector.quantize_mx(
                    out=codes[:, c : c + step].bitcast(FP8X4),
                    scales=scales[:, c : c + step],
                    in_=values[:, PACK * c : PACK * (c + step)],
                )
            return codes, scales

        def prepare_w1(g):
            grouped = keep.tile([P, H * PACK], BF16, name="w1_grouped%d" % g, align_bytes=64)
            dst = grouped[:].rearrange("p (t m j) -> p m t j", t=PACK, j=PACK)
            src = [raw[:].rearrange("p j (m t) -> p m t j", t=PACK) for raw in w1_raw[g]]
            if g == 0:
                nc.scalar.copy(out=dst, in_=src[0])
            else:
                nc.scalar.copy(out=dst[:, 0 : P // 2], in_=src[0])
                nc.vector.tensor_copy(out=dst[:, P // 2 : P // 2 + VECTOR_SHARE], in_=src[1][:, 0:VECTOR_SHARE])
                nc.scalar.copy(out=dst[:, P // 2 + VECTOR_SHARE : P], in_=src[1][:, VECTOR_SHARE : P // 2])
            return quantize("w1q%d" % g, grouped, H, P if g == PASSES - 1 else H)

        def interleaved(grouped, raw):
            return (
                grouped[:].rearrange("p (c i j) -> p c j i", i=4, j=PACK),
                raw[:].rearrange("p j (c i) -> p c j i", i=4),
            )

        def prepare_wv():
            wv_grouped = keep.tile([P, Z * PACK], BF16, name="wv_grouped", align_bytes=64)
            dst, src = interleaved(wv_grouped, wv_raw)
            nc.scalar.activation(out=dst, in_=src, func=ACT.Copy, scale=-4.0)
            return quantize("wvq", wv_grouped, Z, Z)

        x_scale = gather("x_scale", scale_window, U8)
        hidden = [psum.tile([P, PACK, P], F32, name="hidden%d" % i, tag="bank%d" % i) for i in range(TILES)]
        for g in range(PASSES):
            x_codes = gather("x_codes%d" % g, x_window[g], U32)
            w1_codes, w1_scales = prepare_w1(g)
            for i in range(TILES):
                tokens = slice(i * P, (i + 1) * P)
                for t in range(PACK):
                    cols = slice(t * P, (t + 1) * P)
                    nc.tensor.matmul_mx(
                        out=hidden[i][:, t, :],
                        lhsT=w1_codes[:, cols].bitcast(FP8X4),
                        lhsT_scale=w1_scales[:, cols],
                        rhs=x_codes[:, tokens].bitcast(FP8X4),
                        rhs_scale=x_scale[4 * g : P, tokens],
                        start=(g == 0 and t == 0),
                        stop=(g == PASSES - 1 and t == PACK - 1),
                    )

        def cast_wa(u):
            grouped = keep.tile([P, HALF * PACK], BF16, name="wa_grouped%d" % u, align_bytes=64)
            dst, src = interleaved(grouped, wa_raw[u])
            nc.vector.tensor_copy(out=dst, in_=src)
            return grouped

        def quantize_hidden(k, stage, tag=None):
            for j in range(2):
                nc.scalar.activation(
                    out=stage[:, j * K_PASS : (j + 1) * K_PASS].rearrange("p (n t) -> p n t", t=PACK),
                    in_=hidden[2 * k + j][:].rearrange("p t n -> p n t"),
                    func=ACT.Relu,
                )
            h_q.append(quantize("hq%d" % k, stage, 2 * P, 2 * P, tag))

        def products(k, name, bank, width, terms):
            h_codes, h_scales = h_q[k]
            acc = psum.tile([P, 2, width], F32, name="%s%d" % (name, k), tag="bank%d" % bank)
            for j in range(2):
                tokens = slice(j * P, (j + 1) * P)
                for n, ((codes, scales), first) in enumerate(terms):
                    nc.tensor.matmul_mx(
                        out=acc[:, j, :],
                        lhsT=h_codes[:, tokens].bitcast(FP8X4),
                        lhsT_scale=h_scales[:, tokens],
                        rhs=codes[:, first : first + width].bitcast(FP8X4),
                        rhs_scale=scales[:, first : first + width],
                        start=(n == 0),
                        stop=(n == len(terms) - 1),
                    )
            return acc

        def front(k):
            a01[k] = products(k, "a01_", HEAD_BANKS[k][0], HALF, [(wa_q[0], 0)])
            quarter[k] = keep.tile([P, 2, Z], F32, name="quarter%d" % k)
            nc.scalar.activation(out=quarter[k][:], in_=a01[k][:, :, 0:Z], func=ACT.Copy, scale=-0.25)

        def back(k):
            a23[k] = products(k, "a23_", HEAD_BANKS[k][1], HALF, [(wa_q[1], 0)])

        def linear(k):
            terms = [(wv_q, 0), (wa_q[0], Z), (wa_q[1], 0), (wa_q[1], Z)]
            if k == PAIRS - 1:
                terms.append((wa_q[0], 0))
            rest[k] = products(k, "rest", HEAD_BANKS[k][2], Z, terms)

        def max_step(k, action):
            new = keep.tile([P, 2, Z], F32, name="best%d%d" % (k, action))
            if action == 1:
                nc.vector.scalar_tensor_tensor(new[:], quarter[k][:], -4.0, a01[k][:, :, Z : 2 * Z], ALU.mult, ALU.max)
            else:
                cols = slice((action - 2) * Z, (action - 1) * Z)
                nc.vector.tensor_tensor(new[:], a23[k][:, :, cols], best[k][:], ALU.max)
            best[k] = new

        def shift_of(k):
            shift[k] = keep.tile([P, 2, Z], F32, name="shift%d" % k)
            nc.vector.scalar_tensor_tensor(shift[k][:], rest[k][:], -0.25, quarter[k][:], ALU.mult, ALU.add)

        def finish(k):
            result = keep.tile([P, 2, Z], F32, name="result%d" % k)
            if k == PAIRS - 1:
                nc.vector.scalar_tensor_tensor(result[:], rest[k][:], -0.25, best[k][:], ALU.mult, ALU.add)
            else:
                nc.vector.tensor_tensor(result[:], best[k][:], shift[k][:], ALU.add)
            nc.sync.dma_start(
                out=out[2 * k * P : 2 * (k + 1) * P, :].rearrange("(j p) z -> p j z", p=P),
                in_=result[:],
            )

        h_q, a01, a23, rest, quarter, best, shift = [], {}, {}, {}, {}, {}, {}
        wa_first = cast_wa(0)
        wv_q = prepare_wv()
        wa_q = [quantize("waq0", wa_first, HALF, HALF)]
        stage0 = keep.tile([P, 2 * K_PASS], BF16, name="stage0", align_bytes=64)
        quantize_hidden(0, stage0)
        front(0)
        wa_q.append(quantize("waq1", cast_wa(1), HALF, HALF))
        back(0)
        linear(0)
        max_step(0, 1)
        stage1 = keep.tile([P, 2 * K_PASS], BF16, name="stage1", align_bytes=64)
        quantize_hidden(1, stage1, "wa_grouped1")
        front(1)
        back(1)
        max_step(0, 2)
        shift_of(0)
        max_step(0, 3)
        max_step(1, 1)
        finish(0)
        max_step(1, 2)
        stage23 = keep.tile([P, 2, 2 * K_PASS], BF16, name="stage23", tag="stage1", align_bytes=64)
        quantize_hidden(2, stage23[:, 0, :])
        linear(1)
        front(2)
        back(2)
        max_step(1, 3)
        shift_of(1)
        quantize_hidden(3, stage23[:, 1, :])
        front(3)
        linear(2)
        back(3)
        linear(3)
        max_step(2, 1)
        finish(1)
        max_step(2, 2)
        max_step(3, 1)
        max_step(2, 3)
        max_step(3, 2)
        shift_of(2)
        max_step(3, 3)
        finish(2)
        finish(3)
